import numpy as np
import ml_dtypes


def mxq(x, axis, fmt="e4m3"):
    dtype, down = {"e4m3": (ml_dtypes.float8_e4m3fn, 7), "e5m2": (ml_dtypes.float8_e5m2, 14)}[fmt]
    v = np.moveaxis(np.asarray(x, np.float32).astype(ml_dtypes.bfloat16).astype(np.float64), axis, -1)
    blocks = v.reshape(v.shape[:-1] + (-1, 32))
    amax = np.abs(blocks).max(-1, keepdims=True)
    byte = np.maximum(np.where(amax > 0, np.frexp(amax)[1] - 1 + 127, 0) - down, 1)
    scale = np.exp2(byte - 127.0)
    codes = (blocks / scale).astype(np.float32).astype(dtype).astype(np.float64)
    return np.moveaxis((codes * scale).reshape(v.shape), -1, axis)


WIDE = False


def mx_kscale(k):
    if not WIDE:
        return np.ones(k)
    levels = np.array([10, -10, 5, -5, 0])
    if k % 512:
        return np.exp2(np.random.permutation(np.resize(levels, k // 32))).repeat(32)
    a = np.empty((k // 512, 16))
    for p in range(k // 512):
        a[p, :8] = np.random.permutation(np.resize(levels, 8))
        for g in range(8):
            far = levels[np.abs(levels - a[p, g]) >= 10]
            a[p, g + 8] = far[np.random.randint(len(far))]
    return np.exp2(a.ravel()).repeat(32)


def f64(x):
    return np.asarray(x).astype(np.float64)


def striped(idx):
    return np.tile(idx.reshape(-1, 16).T, (8, 1)).astype(np.uint16)


def unstriped(offs):
    return offs[:16].T.reshape(-1).astype(np.int64)


E2M1 = np.array([0.0, 0.5, 1.0, 1.5, 2.0, 3.0, 4.0, 6.0, -0.0, -0.5, -1.0, -1.5, -2.0, -3.0, -4.0, -6.0])


def pack_weight(w, fmt):
    k, n = w.shape
    w = f64(np.asarray(w, np.float32).astype(ml_dtypes.bfloat16)).reshape(k // 32, 32, n)
    amax = np.abs(w).max(1)
    if fmt == "e4m3":
        byte = np.frexp(amax)[1] - 1 + 127 - 7
    else:
        mant, ex = np.frexp(amax / 6.0)
        byte = np.where(mant > 0.5, ex, ex - 1) + 127
    byte = np.clip(np.where(amax > 0, byte, 1), 1, 254)
    scaled = (w * np.exp2(127.0 - byte)[:, None, :]).reshape(k, n).astype(np.float32)
    by_word = np.ascontiguousarray(scaled.reshape(k // 512, 128, 4, n).transpose(0, 1, 3, 2))
    if fmt == "e4m3":
        words = by_word.astype(ml_dtypes.float8_e4m3fn).view(np.uint8)
    else:
        c = by_word.astype(ml_dtypes.float4_e2m1fn).view(np.uint8) & 0xF
        words = (c[..., 0::2] | (c[..., 1::2] << 4)).reshape(k // 512, 128, 2 * n)
    return np.ascontiguousarray(words), np.ascontiguousarray(byte.astype(np.uint8).reshape(k // 512, 16, n))


def unpack_weight(words, scales, fmt):
    g, _, n = scales.shape
    words = np.ascontiguousarray(words).reshape(g, 128, n, -1)
    if fmt == "e4m3":
        vals = words.view(ml_dtypes.float8_e4m3fn).astype(np.float64)
    else:
        nib = np.empty((g, 128, n, 4), np.uint8)
        nib[..., 0::2] = words & 0xF
        nib[..., 1::2] = words >> 4
        vals = E2M1[nib]
    vals = vals * np.repeat(np.exp2(scales.astype(np.float64) - 127.0), 8, axis=1)[..., None]
    return vals.transpose(0, 1, 3, 2).reshape(g * 512, n)


def gelu(v):
    return 0.5 * v * (1.0 + np.tanh(np.sqrt(2.0 / np.pi) * (v + 0.044715 * v**3)))


K, T, S, H, N = 1024, 2048, 512, 1024, 512


def setup_inputs():
    n = np.random.standard_normal
    s = mx_kscale(K)[:, None]
    u = mx_kscale(H)[:, None]
    tab_words, tab_scales = pack_weight(n((K, T)) * s, "e4m3")
    ws_words, ws_scales = pack_weight(n((K, H)) / np.sqrt(K) / s, "e2m1")
    return {
        "tab_words": tab_words, "tab_scales": tab_scales,
        "offs": striped(np.random.permutation(T)[:S]),
        "offs2": striped(np.random.permutation(T)[:S]),
        "offs3": striped(np.random.permutation(T)[:S]),
        "wm": (n((K, H)) / np.sqrt(K) / s).astype(np.float32),
        "ws_words": ws_words, "ws_scales": ws_scales,
        "wr": (n((K, H)) / np.sqrt(K) / s).astype(np.float32),
        "gain": (np.exp(0.3 * n(H)) * u[:, 0]).astype(np.float32),
        "wo": (n((H, N)) / np.sqrt(H) / u).astype(np.float32),
    }


def reference(tab_words, tab_scales, offs, offs2, offs3, wm, ws_words, ws_scales, wr, gain, wo):
    TW = unpack_weight(tab_words, tab_scales, "e4m3")
    v = TW[:, unstriped(offs)]
    v2 = TW[:, unstriped(offs2)]
    v3 = TW[:, unstriped(offs3)]
    wsu = unpack_weight(ws_words, ws_scales, "e2m1")
    mark = mxq(f64(wm), 0, "e4m3").T @ v
    sell = wsu.T @ v2
    part = mxq(f64(wr), 0, "e4m3").T @ v3
    upper = np.maximum(mark, sell)
    lower = np.minimum(sell, part)
    h = f64(gain)[:, None] * (upper * lower)
    out = mxq(f64(wo), 0, "e4m3").T @ mxq(h, 0, "e4m3")
    return out

@@ -1,0 +1,258 @@
+from contextlib import ExitStack
+
+import concourse.mybir as mybir
+
+K, T, S, H, N = 1024, 2048, 512, 1024, 512
+FLOPS = 2 * (3 * K * H * S + H * N * S)
+
+F32 = mybir.dt.float32
+BF16 = mybir.dt.bfloat16
+I32 = mybir.dt.int32
+U32 = mybir.dt.uint32
+U16 = mybir.dt.uint16
+U8 = mybir.dt.uint8
+FP8X4 = mybir.dt.float8_e4m3fn_x4
+FP4X4 = mybir.dt.float4_e2m1fn_x4
+ALU = mybir.AluOpType
+
+P = 128
+PACK = 4
+KP = P * PACK
+HALF = S // 2
+
+
+def tile_list_lot_seller_warnings_kernel(
+    tc, tab_words, tab_scales, offs, offs2, offs3, wm, ws_words, ws_scales, wr, gain, wo, out
+):
+    nc = tc.nc
+    with ExitStack() as ctx:
+        held = ctx.enter_context(tc.tile_pool(name="held", bufs=1))
+        ring = ctx.enter_context(tc.tile_pool(name="ring", bufs=4))
+        psum = ctx.enter_context(tc.psum_pool(name="psum", bufs=1))
+
+        def new(shape, dtype, name):
+            return held.tile(shape, dtype, name=name, align_bytes=64)
+
+        lists = {name: held.tile([P, S // 16], U16, name=name) for name in ("mark_list", "sell_list", "part_list")}
+        tab_w = [new([P, T], I32, "tab_w%d" % a) for a in range(2)]
+        tab_s = new([P, 2, T], U8, "tab_s")
+        ws_w_raw = new([P, 2, 2 * H], U8, "ws_w_raw")
+        ws_s_raw = new([P, 2, H], U8, "ws_s_raw")
+        ws_w = new([P, 2, 2 * H], U8, "ws_w")
+        ws_s = new([P, 2, H], U8, "ws_s")
+        gains = [new([P, PACK], F32, "gains%d" % b) for b in range(2)]
+
+        nc.gpsimd.memset(tab_s[:, 0, :].bitcast(I32), 0)
+        nc.vector.memset(tab_s[:, 1, :].bitcast(I32), 0)
+        nc.gpsimd.memset(ws_s_raw[:].rearrange("p a c -> p (a c)").bitcast(I32), 0)
+
+        def load_planes(tile, planes, q):
+            nc.sync.dma_start(
+                out=tile[32 * q : 32 * q + 4, :, :].bitcast(I32),
+                in_=planes[:, 4 * q : 4 * q + 4, :].rearrange("a r c -> r a c").bitcast(I32),
+            )
+
+        raw = {}
+
+        def load_weight(name, w, a, b):
+            raw[name, a, b] = held.tile([P, PACK, KP], F32, name="raw", bufs=8, align_bytes=64)
+            rows = w[KP * a : KP * (a + 1), KP * b : KP * (b + 1)]
+            nc.sync.dma_start(out=raw[name, a, b][:], in_=rows.rearrange("(p j) c -> p j c", j=PACK))
+
+        def load_table(a):
+            nc.sync.dma_start(out=tab_w[a][:], in_=tab_words[a].rearrange("p t i -> p (t i)").bitcast(I32))
+
+        def load_upper_plane(q):
+            nc.sync.dma_start(
+                out=tab_s[32 * q + 4 : 32 * q + 8, 0, :].bitcast(I32),
+                in_=tab_scales[1, 4 * q : 4 * q + 4, :].bitcast(I32),
+            )
+
+        nc.sync.dma_start(lists["sell_list"][:], offs2)
+        nc.sync.dma_start(lists["mark_list"][:], offs)
+        nc.sync.dma_start(lists["part_list"][:], offs3)
+        for b in range(2):
+            nc.sync.dma_start(out=gains[b][:], in_=gain[KP * b : KP * (b + 1)].rearrange("(p t) -> p t", t=PACK))
+        load_table(0)
+        for a in range(2):
+            nc.sync.dma_start(out=ws_w_raw[:, a, :].bitcast(I32), in_=ws_words[a].bitcast(I32))
+        for q in range(4):
+            load_planes(tab_s, tab_scales, q)
+        load_table(1)
+        for q in range(2):
+            load_upper_plane(q)
+        load_weight("wm", wm, 0, 0)
+        for q in range(2, 4):
+            load_upper_plane(q)
+        for q in range(2):
+            load_planes(ws_s_raw, ws_scales, q)
+        load_weight("wm", wm, 1, 0)
+        for q in range(2, 4):
+            load_planes(ws_s_raw, ws_scales, q)
+        for name, w, b in (("wr", wr, 0), ("wm", wm, 1), ("wr", wr, 1)):
+            for a in range(2):
+                load_weight(name, w, a, b)
+        for a in range(2):
+            load_weight("wo", wo, a, 0)
+
+        picked_w, picked_s = {}, {}
+
+        def gather_words(name, a):
+            picked_w[name, a] = new([P, S], U32, "%s_w%d" % (name, a))
+            nc.vector.tensor_copy(picked_w[name, a][:], tab_w[a][:].bitcast(U32).indirect(lists[name + "_list"][:]))
+
+        def gather_scales(name, window, made):
+            picked_s[made] = new([P, S], U8, made + "_s")
+            nc.vector.tensor_copy(picked_s[made][:], window.indirect(lists[name + "_list"][:]))
+
+        codes, scales = {}, {}
+
+        def copy_on(engine, dst, src):
+            if engine == "v":
+                nc.vector.tensor_copy(out=dst, in_=src)
+            else:
+                nc.scalar.copy(out=dst, in_=src)
+
+        def quantise_weight(name, a, b, engines):
+            grouped = ring.tile([P, PACK * KP], BF16, name="grouped", align_bytes=64)
+            if name == "wo":
+                dst = grouped[:].rearrange("p (m i j) -> p m j i", i=4, j=PACK)
+                src = raw[name, a, b][:].rearrange("p j (m i) -> p m j i", i=4)
+            else:
+                dst = grouped[:].rearrange("p (t m j) -> p m j t", t=PACK, j=PACK)
+                src = raw[name, a, b][:].rearrange("p j (m t) -> p m j t", t=PACK)
+            share = P // len(engines)
+            for u, engine in enumerate(engines):
+                copy_on(engine, dst[:, u * share : (u + 1) * share], src[:, u * share : (u + 1) * share])
+            codes[name, a, b] = new([P, KP], U32, "codes_%s%d%d" % (name, a, b))
+            scales[name, a, b] = new([P, KP], U8, "scales_%s%d%d" % (name, a, b))
+            nc.vector.quantize_mx(out=codes[name, a, b][:].bitcast(FP8X4), scales=scales[name, a, b][:], in_=grouped[:])
+
+        def first_product(dst, name, b, t, cols):
+            for a in range(2):
+                if name == "sell":
+                    c0 = KP * b + P * t
+                    lhs = ws_w[:, a, 2 * c0 : 2 * (c0 + P)].bitcast(FP4X4)
+                    lhs_scale = ws_s[:, a, c0 : c0 + P]
+                    rhs_scale = picked_s["sell%d" % a][:, cols]
+                else:
+                    w = "wm" if name == "mark" else "wr"
+                    lhs = codes[w, a, b][:, P * t : P * (t + 1)].bitcast(FP8X4)
+                    lhs_scale = scales[w, a, b][:, P * t : P * (t + 1)]
+                    rhs_scale = picked_s[name][4 * a :, cols]
+                nc.tensor.matmul_mx(
+                    out=dst, lhsT=lhs, lhsT_scale=lhs_scale,
+                    rhs=picked_w[name, a][:, cols].bitcast(FP8X4), rhs_scale=rhs_scale,
+                    start=(a == 0), stop=(a == 1),
+                )
+
+        def bank():
+            return psum.tile([P, S], F32, name="bank", bufs=4)
+
+        sell = [new([P, PACK, S], F32, "sell%d" % b) for b in range(2)]
+        upper = [new([P, PACK, S], F32, "upper%d" % b) for b in range(2)]
+
+        def sell_half(b):
+            for t in range(PACK):
+                acc = bank()
+                first_product(acc[:], "sell", b, t, slice(0, S))
+                nc.scalar.copy(out=sell[b][:, t, :], in_=acc[:])
+
+        def upper_half(b):
+            for t in range(PACK):
+                acc = bank()
+                first_product(acc[:], "mark", b, t, slice(0, S))
+                nc.vector.tensor_tensor(upper[b][:, t, :], acc[:], sell[b][:, t, :], ALU.max)
+
+        h_codes, h_scales = {}, {}
+
+        def hidden(b, j0, width, engine):
+            cols = slice(j0, j0 + width)
+            per_bank = S // width
+            lower = new([P, PACK, width], F32, "lower%d_%d" % (b, j0))
+            planes = new([P, PACK, width], BF16, "planes%d_%d" % (b, j0))
+            for t0 in range(0, PACK, per_bank):
+                acc = bank()
+                for u in range(per_bank):
+                    first_product(acc[:, u * width : (u + 1) * width], "part", b, t0 + u, cols)
+                nc.vector.tensor_tensor(
+                    lower[:, t0 : t0 + per_bank, :], acc[:].rearrange("p (u c) -> p u c", u=per_bank),
+                    sell[b][:, t0 : t0 + per_bank, cols], ALU.min,
+                )
+            for t in range(PACK):
+                nc.vector.scalar_tensor_tensor(
+                    planes[:, t, :], upper[b][:, t, cols], gains[b][:, t : t + 1], lower[:, t, :], ALU.mult, ALU.mult
+                )
+            woven = new([P, PACK * width], BF16, "woven%d_%d" % (b, j0))
+            copy_on(
+                engine,
+                woven[:].rearrange("p (c i t) -> p c t i", i=4, t=PACK),
+                planes[:].rearrange("p t (c i) -> p c t i", i=4),
+            )
+            made_codes = new([P, width], U32, "h_codes%d_%d" % (b, j0))
+            made_scales = new([P, width], U8, "h_scales%d_%d" % (b, j0))
+            nc.vector.quantize_mx(out=made_codes[:].bitcast(FP8X4), scales=made_scales[:], in_=woven[:])
+            for u in range(width // HALF):
+                h_codes[b, j0 // HALF + u] = made_codes[:, u * HALF : (u + 1) * HALF]
+                h_scales[b, j0 // HALF + u] = made_scales[:, u * HALF : (u + 1) * HALF]
+
+        out_banks = {(jh, n2): psum.tile([P, 2, HALF], F32, name="out%d%d" % (jh, n2)) for jh in range(2) for n2 in range(2)}
+
+        def second_product(b, jh):
+            for n2 in range(2):
+                for u in range(2):
+                    n_cols = slice(P * (2 * n2 + u), P * (2 * n2 + u + 1))
+                    nc.tensor.matmul_mx(
+                        out=out_banks[jh, n2][:, u, :],
+                        lhsT=codes["wo", b, 0][:, n_cols].bitcast(FP8X4), lhsT_scale=scales["wo", b, 0][:, n_cols],
+                        rhs=h_codes[b, jh].bitcast(FP8X4), rhs_scale=h_scales[b, jh],
+                        start=(b == 0 and u == 0), stop=(b == 1 and u == 1),
+                    )
+
+        def store(jh, engines):
+            for n2 in range(2):
+                result = new([P, 2, HALF], F32, "result%d%d" % (jh, n2))
+                copy_on(engines[n2], result[:], out_banks[jh, n2][:])
+                rows = out[2 * P * n2 : 2 * P * (n2 + 1), HALF * jh : HALF * (jh + 1)]
+                nc.sync.dma_start(out=rows.rearrange("(u p) c -> p u c", u=2), in_=result[:])
+
+        for name in ("sell", "mark", "part"):
+            gather_words(name, 0)
+        gather_scales("sell", tab_s[:, 1, :], "sell1")
+        nc.vector.tensor_copy(
+            out=ws_w[:].rearrange("p a c -> p (a c)").bitcast(U16).rearrange("p (g t m) -> p g t m", g=4, t=PACK),
+            in_=ws_w_raw[:].rearrange("p a c -> p (a c)").bitcast(U16).rearrange("p (g m t) -> p g t m", g=4, t=PACK),
+        )
+
+        for name in ("sell", "mark", "part"):
+            gather_words(name, 1)
+        gather_scales("sell", tab_s[:, 0, :], "sell0")
+        nc.vector.tensor_copy(
+            out=ws_s[:].rearrange("p a (b t m) -> p (a b) t m", b=2, t=PACK),
+            in_=ws_s_raw[:].rearrange("p a (b m t) -> p (a b) t m", b=2, t=PACK),
+        )
+        quantise_weight("wm", 0, 0, "s")
+        gather_scales("mark", tab_s[:, 0, :], "mark")
+        quantise_weight("wm", 1, 0, "s")
+        sell_half(0)
+        gather_scales("part", tab_s[:, 0, :], "part")
+        quantise_weight("wr", 0, 0, "s")
+        upper_half(0)
+        quantise_weight("wr", 1, 0, "s")
+        sell_half(1)
+        quantise_weight("wm", 0, 1, "s")
+        hidden(0, 0, S, "s")
+        quantise_weight("wm", 1, 1, "s")
+        upper_half(1)
+        quantise_weight("wr", 0, 1, "s")
+        quantise_weight("wr", 1, 1, "s")
+        quantise_weight("wo", 0, 0, "s")
+        hidden(1, 0, HALF, "s")
+        quantise_weight("wo", 1, 0, "s")
+        second_product(0, 0)
+        second_product(0, 1)
+        hidden(1, HALF, HALF, "v")
+        second_product(1, 0)
+        store(0, "ss")
+        second_product(1, 1)
+        store(1, "sv")

@@ -1,6 +1,7 @@
 from contextlib import ExitStack
 
 import concourse.mybir as mybir
+from concourse.masks import make_identity
 
 K, T, S, H, N = 1024, 2048, 512, 1024, 512
 FLOPS = 2 * (3 * K * H * S + H * N * S)
@@ -40,11 +41,15 @@ def tile_list_lot_seller_warnings_kernel(
         ws_s_raw = new([P, 2, H], U8, "ws_s_raw")
         ws_w = new([P, 2, 2 * H], U8, "ws_w")
         ws_s = new([P, 2, H], U8, "ws_s")
-        gains = [new([P, PACK], F32, "gains%d" % b) for b in range(2)]
+        gains = new([P, 2 * PACK], F32, "gains")
+        gain_rows = new([P, P], F32, "gain_rows")
+        identity = new([P, P], F32, "identity")
 
         nc.gpsimd.memset(tab_s[:, 0, :].bitcast(I32), 0)
         nc.vector.memset(tab_s[:, 1, :].bitcast(I32), 0)
         nc.gpsimd.memset(ws_s_raw[:].rearrange("p a c -> p (a c)").bitcast(I32), 0)
+        nc.gpsimd.memset(gain_rows[:], 0.0)
+        make_identity(nc, identity[:])
 
         def load_planes(tile, planes, q):
             nc.sync.dma_start(
@@ -57,7 +62,19 @@ def tile_list_lot_seller_warnings_kernel(
         def load_weight(name, w, a, b):
             raw[name, a, b] = held.tile([P, PACK, KP], F32, name="raw", bufs=8, align_bytes=64)
             rows = w[KP * a : KP * (a + 1), KP * b : KP * (b + 1)]
-            nc.sync.dma_start(out=raw[name, a, b][:], in_=rows.rearrange("(p j) c -> p j c", j=PACK))
+            if name == "wo":
+                for t in range(PACK):
+                    nc.sync.dma_start(
+                        out=raw[name, a, b][:, t, :], in_=rows.rearrange("(q t i) c -> t q i c", t=PACK, i=8)[t]
+                    )
+            else:
+                nc.sync.dma_start(out=raw[name, a, b][:], in_=rows.rearrange("(p j) c -> p j c", j=PACK))
+
+        def load_gain(b):
+            nc.sync.dma_start(
+                out=gain_rows[PACK * b : PACK * (b + 1), :].rearrange("t (q i) -> t q i", i=8),
+                in_=gain[KP * b : KP * (b + 1)].rearrange("(q t i) -> t q i", t=PACK, i=8),
+            )
 
         def load_table(a):
             nc.sync.dma_start(out=tab_w[a][:], in_=tab_words[a].rearrange("p t i -> p (t i)").bitcast(I32))
@@ -69,26 +86,21 @@ def tile_list_lot_seller_warnings_kernel(
             )
 
         nc.sync.dma_start(lists["sell_list"][:], offs2)
-        nc.sync.dma_start(lists["mark_list"][:], offs)
-        nc.sync.dma_start(lists["part_list"][:], offs3)
-        for b in range(2):
-            nc.sync.dma_start(out=gains[b][:], in_=gain[KP * b : KP * (b + 1)].rearrange("(p t) -> p t", t=PACK))
         load_table(0)
-        for a in range(2):
-            nc.sync.dma_start(out=ws_w_raw[:, a, :].bitcast(I32), in_=ws_words[a].bitcast(I32))
+        nc.sync.dma_start(lists["mark_list"][:], offs)
+        nc.sync.dma_start(out=ws_w_raw[:].bitcast(I32), in_=ws_words.rearrange("a p c -> p a c").bitcast(I32))
         for q in range(4):
             load_planes(tab_s, tab_scales, q)
         load_table(1)
-        for q in range(2):
-            load_upper_plane(q)
+        for q in range(4):
+            load_planes(ws_s_raw, ws_scales, q)
         load_weight("wm", wm, 0, 0)
-        for q in range(2, 4):
+        for q in range(4):
             load_upper_plane(q)
-        for q in range(2):
-            load_planes(ws_s_raw, ws_scales, q)
         load_weight("wm", wm, 1, 0)
-        for q in range(2, 4):
-            load_planes(ws_s_raw, ws_scales, q)
+        nc.sync.dma_start(lists["part_list"][:], offs3)
+        for b in range(2):
+            load_gain(b)
         for name, w, b in (("wr", wr, 0), ("wm", wm, 1), ("wr", wr, 1)):
             for a in range(2):
                 load_weight(name, w, a, b)
@@ -118,12 +130,12 @@ def tile_list_lot_seller_warnings_kernel(
             if name == "wo":
                 dst = grouped[:].rearrange("p (m i j) -> p m j i", i=4, j=PACK)
                 src = raw[name, a, b][:].rearrange("p j (m i) -> p m j i", i=4)
+                copy_on(engines[0], dst, src)
             else:
-                dst = grouped[:].rearrange("p (t m j) -> p m j t", t=PACK, j=PACK)
-                src = raw[name, a, b][:].rearrange("p j (m t) -> p m j t", t=PACK)
-            share = P // len(engines)
-            for u, engine in enumerate(engines):
-                copy_on(engine, dst[:, u * share : (u + 1) * share], src[:, u * share : (u + 1) * share])
+                dst = grouped[:].rearrange("p (t q h i j) -> p t q h j i", t=PACK, h=2, i=4, j=PACK)
+                src = raw[name, a, b][:].rearrange("p j (q t h i) -> p t q h j i", t=PACK, h=2, i=4)
+                for t in range(PACK):
+                    copy_on(engines[t % len(engines)], dst[:, t], src[:, t])
             codes[name, a, b] = new([P, KP], U32, "codes_%s%d%d" % (name, a, b))
             scales[name, a, b] = new([P, KP], U8, "scales_%s%d%d" % (name, a, b))
             nc.vector.quantize_mx(out=codes[name, a, b][:].bitcast(FP8X4), scales=scales[name, a, b][:], in_=grouped[:])
@@ -147,7 +159,7 @@ def tile_list_lot_seller_warnings_kernel(
                 )
 
         def bank():
-            return psum.tile([P, S], F32, name="bank", bufs=4)
+            return psum.tile([P, S], F32, name="bank", bufs=8)
 
         sell = [new([P, PACK, S], F32, "sell%d" % b) for b in range(2)]
         upper = [new([P, PACK, S], F32, "upper%d" % b) for b in range(2)]
@@ -181,7 +193,7 @@ def tile_list_lot_seller_warnings_kernel(
                 )
             for t in range(PACK):
                 nc.vector.scalar_tensor_tensor(
-                    planes[:, t, :], upper[b][:, t, cols], gains[b][:, t : t + 1], lower[:, t, :], ALU.mult, ALU.mult
+                    planes[:, t, :], upper[b][:, t, cols], gains[:, PACK * b + t : PACK * b + t + 1], lower[:, t, :], ALU.mult, ALU.mult
                 )
             woven = new([P, PACK * width], BF16, "woven%d_%d" % (b, j0))
             copy_on(
@@ -192,67 +204,79 @@ def tile_list_lot_seller_warnings_kernel(
             made_codes = new([P, width], U32, "h_codes%d_%d" % (b, j0))
             made_scales = new([P, width], U8, "h_scales%d_%d" % (b, j0))
             nc.vector.quantize_mx(out=made_codes[:].bitcast(FP8X4), scales=made_scales[:], in_=woven[:])
-            for u in range(width // HALF):
-                h_codes[b, j0 // HALF + u] = made_codes[:, u * HALF : (u + 1) * HALF]
-                h_scales[b, j0 // HALF + u] = made_scales[:, u * HALF : (u + 1) * HALF]
+            h_codes[b, j0], h_scales[b, j0] = made_codes, made_scales
 
-        out_banks = {(jh, n2): psum.tile([P, 2, HALF], F32, name="out%d%d" % (jh, n2)) for jh in range(2) for n2 in range(2)}
+        out_banks = {}
 
-        def second_product(b, jh):
-            for n2 in range(2):
-                for u in range(2):
-                    n_cols = slice(P * (2 * n2 + u), P * (2 * n2 + u + 1))
+        def second_product(b, j0, width):
+            per_bank = S // width
+            made_at = j0 if b == 1 else 0
+            cols = slice(j0 - made_at, j0 - made_at + width)
+            for n0 in range(0, N // P, per_bank):
+                if b == 0:
+                    out_banks[j0, n0] = bank()[:].rearrange("p (u c) -> p u c", u=per_bank)
+                for u in range(per_bank):
+                    n_cols = slice(P * (n0 + u), P * (n0 + u + 1))
                     nc.tensor.matmul_mx(
-                        out=out_banks[jh, n2][:, u, :],
+                        out=out_banks[j0, n0][:, u, :],
                         lhsT=codes["wo", b, 0][:, n_cols].bitcast(FP8X4), lhsT_scale=scales["wo", b, 0][:, n_cols],
-                        rhs=h_codes[b, jh].bitcast(FP8X4), rhs_scale=h_scales[b, jh],
-                        start=(b == 0 and u == 0), stop=(b == 1 and u == 1),
+                        rhs=h_codes[b, made_at][:, cols].bitcast(FP8X4), rhs_scale=h_scales[b, made_at][:, cols],
+                        start=(b == 0 and u == 0), stop=(b == 1 and u == per_bank - 1),
                     )
 
-        def store(jh, engines):
-            for n2 in range(2):
-                result = new([P, 2, HALF], F32, "result%d%d" % (jh, n2))
-                copy_on(engines[n2], result[:], out_banks[jh, n2][:])
-                rows = out[2 * P * n2 : 2 * P * (n2 + 1), HALF * jh : HALF * (jh + 1)]
-                nc.sync.dma_start(out=rows.rearrange("(u p) c -> p u c", u=2), in_=result[:])
+        def store(j0, width, engines):
+            per_bank = S // width
+            for n0, engine in zip(range(0, N // P, per_bank), engines):
+                result = new([P, per_bank, width], F32, "result%d_%d" % (j0, n0))
+                copy_on(engine, result[:], out_banks[j0, n0])
+                rows = out[P * n0 : P * (n0 + per_bank), j0 : j0 + width]
+                nc.sync.dma_start(out=rows.rearrange("(u p) c -> p u c", u=per_bank), in_=result[:])
 
-        for name in ("sell", "mark", "part"):
-            gather_words(name, 0)
+        turned = bank()
+        nc.tensor.transpose(turned[:, 0:P], gain_rows[:], identity[:])
+        nc.scalar.copy(out=gains[:], in_=turned[:, 0 : 2 * PACK])
+
+        gather_words("sell", 0)
+        gather_words("mark", 0)
         gather_scales("sell", tab_s[:, 1, :], "sell1")
         nc.vector.tensor_copy(
-            out=ws_w[:].rearrange("p a c -> p (a c)").bitcast(U16).rearrange("p (g t m) -> p g t m", g=4, t=PACK),
-            in_=ws_w_raw[:].rearrange("p a c -> p (a c)").bitcast(U16).rearrange("p (g m t) -> p g t m", g=4, t=PACK),
+            out=ws_w[:].rearrange("p a c -> p (a c)").bitcast(I32).rearrange("p (g t q i) -> p g t q i", g=4, t=PACK, i=4),
+            in_=ws_w_raw[:].rearrange("p a c -> p (a c)").bitcast(I32).rearrange("p (g q t i) -> p g t q i", g=4, t=PACK, i=4),
         )
-
-        for name in ("sell", "mark", "part"):
-            gather_words(name, 1)
-        gather_scales("sell", tab_s[:, 0, :], "sell0")
+        gather_words("sell", 1)
         nc.vector.tensor_copy(
-            out=ws_s[:].rearrange("p a (b t m) -> p (a b) t m", b=2, t=PACK),
-            in_=ws_s_raw[:].rearrange("p a (b m t) -> p (a b) t m", b=2, t=PACK),
+            out=ws_s[:].rearrange("p a c -> p (a c)").bitcast(I32).rearrange("p (g t q i) -> p g t q i", g=4, t=PACK, i=2),
+            in_=ws_s_raw[:].rearrange("p a c -> p (a c)").bitcast(I32).rearrange("p (g q t i) -> p g t q i", g=4, t=PACK, i=2),
         )
-        quantise_weight("wm", 0, 0, "s")
+        gather_scales("sell", tab_s[:, 0, :], "sell0")
+        gather_words("mark", 1)
         gather_scales("mark", tab_s[:, 0, :], "mark")
+        quantise_weight("wm", 0, 0, "s")
         quantise_weight("wm", 1, 0, "s")
-        sell_half(0)
-        gather_scales("part", tab_s[:, 0, :], "part")
         quantise_weight("wr", 0, 0, "s")
+        sell_half(0)
+        gather_words("part", 0)
+        gather_words("part", 1)
+        gather_scales("part", tab_s[:, 0, :], "part")
         upper_half(0)
-        quantise_weight("wr", 1, 0, "s")
+        quantise_weight("wr", 1, 0, "sv")
         sell_half(1)
-        quantise_weight("wm", 0, 1, "s")
-        hidden(0, 0, S, "s")
-        quantise_weight("wm", 1, 1, "s")
-        upper_half(1)
-        quantise_weight("wr", 0, 1, "s")
+        quantise_weight("wm", 0, 1, "sv")
+        quantise_weight("wm", 1, 1, "sv")
+        quantise_weight("wr", 0, 1, "sv")
         quantise_weight("wr", 1, 1, "s")
+        hidden(0, 0, S, "s")
+        upper_half(1)
         quantise_weight("wo", 0, 0, "s")
-        hidden(1, 0, HALF, "s")
         quantise_weight("wo", 1, 0, "s")
-        second_product(0, 0)
-        second_product(0, 1)
-        hidden(1, HALF, HALF, "v")
-        second_product(1, 0)
-        store(0, "ss")
-        second_product(1, 1)
-        store(1, "sv")
+        hidden(1, 0, 256, "s")
+        for j0, width in ((0, 256), (256, 128), (384, 128)):
+            second_product(0, j0, width)
+        hidden(1, 256, 128, "s")
+        second_product(1, 0, 256)
+        store(0, 256, "ss")
+        second_product(1, 256, 128)
+        store(256, 128, "s")
+        hidden(1, 384, 128, "v")
+        second_product(1, 384, 128)
+        store(384, 128, "v")

@@ -45,16 +45,20 @@ def tile_list_lot_seller_warnings_kernel(
         gain_rows = new([P, P], F32, "gain_rows")
         identity = new([P, P], F32, "identity")
 
-        nc.gpsimd.memset(tab_s[:, 0, :].bitcast(I32), 0)
-        nc.vector.memset(tab_s[:, 1, :].bitcast(I32), 0)
         nc.gpsimd.memset(ws_s_raw[:].rearrange("p a c -> p (a c)").bitcast(I32), 0)
-        nc.gpsimd.memset(gain_rows[:], 0.0)
+        nc.vector.memset(tab_s[:, 0, :].bitcast(I32), 0)
+        nc.vector.memset(tab_s[:, 1, :].bitcast(I32), 0)
+        nc.vector.memset(gain_rows[:], 0.0)
+        for r in range(4):
+            nc.gpsimd.dma_start(
+                out=ws_s_raw[r:P:32, :, :].bitcast(I32),
+                in_=ws_scales.rearrange("a (q r) c -> r q a c", r=4)[r].bitcast(I32),
+            )
         make_identity(nc, identity[:])
-
-        def load_planes(tile, planes, q):
-            nc.sync.dma_start(
-                out=tile[32 * q : 32 * q + 4, :, :].bitcast(I32),
-                in_=planes[:, 4 * q : 4 * q + 4, :].rearrange("a r c -> r a c").bitcast(I32),
+        for q in range(4):
+            nc.gpsimd.dma_start(
+                out=tab_s[32 * q : 32 * q + 8, 0, :].bitcast(I32),
+                in_=tab_scales[:, 4 * q : 4 * q + 4, :].bitcast(I32),
             )
 
         raw = {}
@@ -79,24 +83,17 @@ def tile_list_lot_seller_warnings_kernel(
         def load_table(a):
             nc.sync.dma_start(out=tab_w[a][:], in_=tab_words[a].rearrange("p t i -> p (t i)").bitcast(I32))
 
-        def load_upper_plane(q):
-            nc.sync.dma_start(
-                out=tab_s[32 * q + 4 : 32 * q + 8, 0, :].bitcast(I32),
-                in_=tab_scales[1, 4 * q : 4 * q + 4, :].bitcast(I32),
-            )
-
         nc.sync.dma_start(lists["sell_list"][:], offs2)
         load_table(0)
         nc.sync.dma_start(lists["mark_list"][:], offs)
         nc.sync.dma_start(out=ws_w_raw[:].bitcast(I32), in_=ws_words.rearrange("a p c -> p a c").bitcast(I32))
-        for q in range(4):
-            load_planes(tab_s, tab_scales, q)
+        for r in range(4):
+            nc.sync.dma_start(
+                out=tab_s[r:P:32, 1, :].bitcast(I32),
+                in_=tab_scales[1].rearrange("(q r) c -> r q c", r=4)[r].bitcast(I32),
+            )
         load_table(1)
-        for q in range(4):
-            load_planes(ws_s_raw, ws_scales, q)
         load_weight("wm", wm, 0, 0)
-        for q in range(4):
-            load_upper_plane(q)
         load_weight("wm", wm, 1, 0)
         nc.sync.dma_start(lists["part_list"][:], offs3)
         for b in range(2):

@@ -46,20 +46,10 @@ def tile_list_lot_seller_warnings_kernel(
         identity = new([P, P], F32, "identity")
 
         nc.gpsimd.memset(ws_s_raw[:].rearrange("p a c -> p (a c)").bitcast(I32), 0)
-        nc.vector.memset(tab_s[:, 0, :].bitcast(I32), 0)
         nc.vector.memset(tab_s[:, 1, :].bitcast(I32), 0)
-        nc.vector.memset(gain_rows[:], 0.0)
-        for r in range(4):
-            nc.gpsimd.dma_start(
-                out=ws_s_raw[r:P:32, :, :].bitcast(I32),
-                in_=ws_scales.rearrange("a (q r) c -> r q a c", r=4)[r].bitcast(I32),
-            )
+        nc.gpsimd.memset(tab_s[:, 0, :].bitcast(I32), 0)
+        nc.gpsimd.memset(gain_rows[:], 0.0)
         make_identity(nc, identity[:])
-        for q in range(4):
-            nc.gpsimd.dma_start(
-                out=tab_s[32 * q : 32 * q + 8, 0, :].bitcast(I32),
-                in_=tab_scales[:, 4 * q : 4 * q + 4, :].bitcast(I32),
-            )
 
         raw = {}
 
@@ -83,17 +73,32 @@ def tile_list_lot_seller_warnings_kernel(
         def load_table(a):
             nc.sync.dma_start(out=tab_w[a][:], in_=tab_words[a].rearrange("p t i -> p (t i)").bitcast(I32))
 
+        def load_both_planes(q):
+            nc.sync.dma_start(
+                out=tab_s[32 * q : 32 * q + 8, 0, :].bitcast(I32),
+                in_=tab_scales[:, 4 * q : 4 * q + 4, :].bitcast(I32),
+            )
+
         nc.sync.dma_start(lists["sell_list"][:], offs2)
         load_table(0)
         nc.sync.dma_start(lists["mark_list"][:], offs)
         nc.sync.dma_start(out=ws_w_raw[:].bitcast(I32), in_=ws_words.rearrange("a p c -> p a c").bitcast(I32))
         for r in range(4):
             nc.sync.dma_start(
+                out=ws_s_raw[r:P:32, :, :].bitcast(I32),
+                in_=ws_scales.rearrange("a (q r) c -> r q a c", r=4)[r].bitcast(I32),
+            )
+        load_table(1)
+        for r in range(4):
+            nc.sync.dma_start(
                 out=tab_s[r:P:32, 1, :].bitcast(I32),
                 in_=tab_scales[1].rearrange("(q r) c -> r q c", r=4)[r].bitcast(I32),
             )
-        load_table(1)
+        for q in range(2):
+            load_both_planes(q)
         load_weight("wm", wm, 0, 0)
+        for q in range(2, 4):
+            load_both_planes(q)
         load_weight("wm", wm, 1, 0)
         nc.sync.dma_start(lists["part_list"][:], offs3)
         for b in range(2):
@@ -250,30 +255,27 @@ def tile_list_lot_seller_warnings_kernel(
         gather_scales("mark", tab_s[:, 0, :], "mark")
         quantise_weight("wm", 0, 0, "s")
         quantise_weight("wm", 1, 0, "s")
-        quantise_weight("wr", 0, 0, "s")
+        quantise_weight("wr", 0, 0, "sv")
+        quantise_weight("wr", 1, 0, "sv")
         sell_half(0)
         gather_words("part", 0)
         gather_words("part", 1)
         gather_scales("part", tab_s[:, 0, :], "part")
         upper_half(0)
-        quantise_weight("wr", 1, 0, "sv")
-        sell_half(1)
         quantise_weight("wm", 0, 1, "sv")
         quantise_weight("wm", 1, 1, "sv")
-        quantise_weight("wr", 0, 1, "sv")
+        sell_half(1)
+        quantise_weight("wr", 0, 1, "s")
         quantise_weight("wr", 1, 1, "s")
-        hidden(0, 0, S, "s")
-        upper_half(1)
         quantise_weight("wo", 0, 0, "s")
         quantise_weight("wo", 1, 0, "s")
-        hidden(1, 0, 256, "s")
-        for j0, width in ((0, 256), (256, 128), (384, 128)):
-            second_product(0, j0, width)
-        hidden(1, 256, 128, "s")
-        second_product(1, 0, 256)
-        store(0, 256, "ss")
-        second_product(1, 256, 128)
-        store(256, 128, "s")
-        hidden(1, 384, 128, "v")
-        second_product(1, 384, 128)
-        store(384, 128, "v")
+        hidden(0, 0, S, "s")
+        upper_half(1)
+        hidden(1, 0, HALF, "s")
+        second_product(0, 0, HALF)
+        second_product(0, HALF, HALF)
+        hidden(1, HALF, HALF, "v")
+        second_product(1, 0, HALF)
+        store(0, HALF, "ss")
+        second_product(1, HALF, HALF)
+        store(HALF, HALF, "sv")

@@ -36,7 +36,8 @@ def tile_list_lot_seller_warnings_kernel(
 
         lists = {name: held.tile([P, S // 16], U16, name=name) for name in ("mark_list", "sell_list", "part_list")}
         tab_w = [new([P, T], I32, "tab_w%d" % a) for a in range(2)]
-        tab_s = new([P, 2, T], U8, "tab_s")
+        tab_s = new([P, T], U8, "tab_s")
+        sell_s1 = new([P, S], U8, "sell_s1")
         ws_w_raw = new([P, 2, 2 * H], U8, "ws_w_raw")
         ws_s_raw = new([P, 2, H], U8, "ws_s_raw")
         ws_w = new([P, 2, 2 * H], U8, "ws_w")
@@ -45,9 +46,9 @@ def tile_list_lot_seller_warnings_kernel(
         gain_rows = new([P, P], F32, "gain_rows")
         identity = new([P, P], F32, "identity")
 
-        nc.gpsimd.memset(ws_s_raw[:].rearrange("p a c -> p (a c)").bitcast(I32), 0)
-        nc.vector.memset(tab_s[:, 1, :].bitcast(I32), 0)
-        nc.gpsimd.memset(tab_s[:, 0, :].bitcast(I32), 0)
+        nc.gpsimd.memset(tab_s[:].bitcast(I32), 0)
+        nc.vector.memset(ws_s_raw[:].rearrange("p a c -> p (a c)").bitcast(I32), 0)
+        nc.gpsimd.memset(sell_s1[:].bitcast(I32), 0)
         nc.gpsimd.memset(gain_rows[:], 0.0)
         make_identity(nc, identity[:])
 
@@ -73,34 +74,24 @@ def tile_list_lot_seller_warnings_kernel(
         def load_table(a):
             nc.sync.dma_start(out=tab_w[a][:], in_=tab_words[a].rearrange("p t i -> p (t i)").bitcast(I32))
 
-        def load_both_planes(q):
-            nc.sync.dma_start(
-                out=tab_s[32 * q : 32 * q + 8, 0, :].bitcast(I32),
-                in_=tab_scales[:, 4 * q : 4 * q + 4, :].bitcast(I32),
-            )
-
         nc.sync.dma_start(lists["sell_list"][:], offs2)
         load_table(0)
         nc.sync.dma_start(lists["mark_list"][:], offs)
+        for q in range(4):
+            nc.sync.dma_start(
+                out=tab_s[32 * q : 32 * q + 8, :].bitcast(I32),
+                in_=tab_scales[:, 4 * q : 4 * q + 4, :].bitcast(I32),
+            )
+        load_table(1)
         nc.sync.dma_start(out=ws_w_raw[:].bitcast(I32), in_=ws_words.rearrange("a p c -> p a c").bitcast(I32))
         for r in range(4):
             nc.sync.dma_start(
                 out=ws_s_raw[r:P:32, :, :].bitcast(I32),
                 in_=ws_scales.rearrange("a (q r) c -> r q a c", r=4)[r].bitcast(I32),
             )
-        load_table(1)
-        for r in range(4):
-            nc.sync.dma_start(
-                out=tab_s[r:P:32, 1, :].bitcast(I32),
-                in_=tab_scales[1].rearrange("(q r) c -> r q c", r=4)[r].bitcast(I32),
-            )
-        for q in range(2):
-            load_both_planes(q)
         load_weight("wm", wm, 0, 0)
-        for q in range(2, 4):
-            load_both_planes(q)
-        load_weight("wm", wm, 1, 0)
         nc.sync.dma_start(lists["part_list"][:], offs3)
+        load_weight("wm", wm, 1, 0)
         for b in range(2):
             load_gain(b)
         for name, w, b in (("wr", wr, 0), ("wm", wm, 1), ("wr", wr, 1)):
@@ -115,9 +106,9 @@ def tile_list_lot_seller_warnings_kernel(
             picked_w[name, a] = new([P, S], U32, "%s_w%d" % (name, a))
             nc.vector.tensor_copy(picked_w[name, a][:], tab_w[a][:].bitcast(U32).indirect(lists[name + "_list"][:]))
 
-        def gather_scales(name, window, made):
-            picked_s[made] = new([P, S], U8, made + "_s")
-            nc.vector.tensor_copy(picked_s[made][:], window.indirect(lists[name + "_list"][:]))
+        def gather_scales(name):
+            picked_s[name] = new([P, S], U8, name + "_s")
+            nc.vector.tensor_copy(picked_s[name][:], tab_s[:].indirect(lists[name + "_list"][:]))
 
         codes, scales = {}, {}
 
@@ -148,7 +139,7 @@ def tile_list_lot_seller_warnings_kernel(
                     c0 = KP * b + P * t
                     lhs = ws_w[:, a, 2 * c0 : 2 * (c0 + P)].bitcast(FP4X4)
                     lhs_scale = ws_s[:, a, c0 : c0 + P]
-                    rhs_scale = picked_s["sell%d" % a][:, cols]
+                    rhs_scale = (picked_s["sell"], sell_s1)[a][:, cols]
                 else:
                     w = "wm" if name == "mark" else "wr"
                     lhs = codes[w, a, b][:, P * t : P * (t + 1)].bitcast(FP8X4)
@@ -239,38 +230,38 @@ def tile_list_lot_seller_warnings_kernel(
         nc.scalar.copy(out=gains[:], in_=turned[:, 0 : 2 * PACK])
 
         gather_words("sell", 0)
+        gather_scales("sell")
+        nc.scalar.dma_start(out=sell_s1[0:100, :].bitcast(I32), in_=picked_s["sell"][4:104, :].bitcast(I32))
         gather_words("mark", 0)
-        gather_scales("sell", tab_s[:, 1, :], "sell1")
+        gather_words("sell", 1)
         nc.vector.tensor_copy(
             out=ws_w[:].rearrange("p a c -> p (a c)").bitcast(I32).rearrange("p (g t q i) -> p g t q i", g=4, t=PACK, i=4),
             in_=ws_w_raw[:].rearrange("p a c -> p (a c)").bitcast(I32).rearrange("p (g q t i) -> p g t q i", g=4, t=PACK, i=4),
         )
-        gather_words("sell", 1)
         nc.vector.tensor_copy(
             out=ws_s[:].rearrange("p a c -> p (a c)").bitcast(I32).rearrange("p (g t q i) -> p g t q i", g=4, t=PACK, i=2),
             in_=ws_s_raw[:].rearrange("p a c -> p (a c)").bitcast(I32).rearrange("p (g q t i) -> p g t q i", g=4, t=PACK, i=2),
         )
-        gather_scales("sell", tab_s[:, 0, :], "sell0")
-        gather_words("mark", 1)
-        gather_scales("mark", tab_s[:, 0, :], "mark")
-        quantise_weight("wm", 0, 0, "s")
-        quantise_weight("wm", 1, 0, "s")
-        quantise_weight("wr", 0, 0, "sv")
-        quantise_weight("wr", 1, 0, "sv")
-        sell_half(0)
         gather_words("part", 0)
+        gather_words("mark", 1)
+        gather_scales("mark")
         gather_words("part", 1)
-        gather_scales("part", tab_s[:, 0, :], "part")
+        quantise_weight("wm", 0, 0, "s")
+        quantise_weight("wm", 1, 0, "sv")
+        quantise_weight("wr", 0, 0, "sv")
+        sell_half(0)
+        gather_scales("part")
         upper_half(0)
+        quantise_weight("wr", 1, 0, "sv")
+        sell_half(1)
         quantise_weight("wm", 0, 1, "sv")
         quantise_weight("wm", 1, 1, "sv")
-        sell_half(1)
         quantise_weight("wr", 0, 1, "s")
         quantise_weight("wr", 1, 1, "s")
-        quantise_weight("wo", 0, 0, "s")
-        quantise_weight("wo", 1, 0, "s")
         hidden(0, 0, S, "s")
         upper_half(1)
+        quantise_weight("wo", 0, 0, "s")
+        quantise_weight("wo", 1, 0, "s")
         hidden(1, 0, HALF, "s")
         second_product(0, 0, HALF)
         second_product(0, HALF, HALF)

from contextlib import ExitStack

import concourse.mybir as mybir
from concourse.masks import make_identity

K, T, S, H, N = 1024, 2048, 512, 1024, 512
FLOPS = 2 * (3 * K * H * S + H * N * S)

F32 = mybir.dt.float32
BF16 = mybir.dt.bfloat16
I32 = mybir.dt.int32
U32 = mybir.dt.uint32
U16 = mybir.dt.uint16
U8 = mybir.dt.uint8
FP8X4 = mybir.dt.float8_e4m3fn_x4
FP4X4 = mybir.dt.float4_e2m1fn_x4
ALU = mybir.AluOpType

P = 128
PACK = 4
KP = P * PACK
HALF = S // 2


def tile_list_lot_seller_warnings_kernel(
    tc, tab_words, tab_scales, offs, offs2, offs3, wm, ws_words, ws_scales, wr, gain, wo, out
):
    nc = tc.nc
    with ExitStack() as ctx:
        held = ctx.enter_context(tc.tile_pool(name="held", bufs=1))
        ring = ctx.enter_context(tc.tile_pool(name="ring", bufs=4))
        psum = ctx.enter_context(tc.psum_pool(name="psum", bufs=1))

        def new(shape, dtype, name):
            return held.tile(shape, dtype, name=name, align_bytes=64)

        lists = {name: held.tile([P, S // 16], U16, name=name) for name in ("mark_list", "sell_list", "part_list")}
        tab_w = [new([P, T], I32, "tab_w%d" % a) for a in range(2)]
        tab_s = new([P, T], U8, "tab_s")
        sell_s1 = new([P, S], U8, "sell_s1")
        ws_w_raw = new([P, 2, 2 * H], U8, "ws_w_raw")
        ws_s_raw = new([P, 2, H], U8, "ws_s_raw")
        ws_w = new([P, 2, 2 * H], U8, "ws_w")
        ws_s = new([P, 2, H], U8, "ws_s")
        gains = new([P, 2 * PACK], F32, "gains")
        gain_rows = new([P, P], F32, "gain_rows")
        identity = new([P, P], F32, "identity")

        nc.gpsimd.memset(tab_s[:].bitcast(I32), 0)
        nc.vector.memset(ws_s_raw[:].rearrange("p a c -> p (a c)").bitcast(I32), 0)
        nc.gpsimd.memset(sell_s1[:].bitcast(I32), 0)
        nc.gpsimd.memset(gain_rows[:], 0.0)
        make_identity(nc, identity[:])

        raw = {}

        def load_weight(name, w, a, b):
            raw[name, a, b] = held.tile([P, PACK, KP], F32, name="raw", bufs=8, align_bytes=64)
            rows = w[KP * a : KP * (a + 1), KP * b : KP * (b + 1)]
            if name == "wo":
                for t in range(PACK):
                    nc.sync.dma_start(
                        out=raw[name, a, b][:, t, :], in_=rows.rearrange("(q t i) c -> t q i c", t=PACK, i=8)[t]
                    )
            else:
                nc.sync.dma_start(out=raw[name, a, b][:], in_=rows.rearrange("(p j) c -> p j c", j=PACK))

        def load_gain(b):
            nc.sync.dma_start(
                out=gain_rows[PACK * b : PACK * (b + 1), :].rearrange("t (q i) -> t q i", i=8),
                in_=gain[KP * b : KP * (b + 1)].rearrange("(q t i) -> t q i", t=PACK, i=8),
            )

        def load_table(a):
            nc.sync.dma_start(out=tab_w[a][:], in_=tab_words[a].rearrange("p t i -> p (t i)").bitcast(I32))

        nc.sync.dma_start(lists["sell_list"][:], offs2)
        load_table(0)
        nc.sync.dma_start(lists["mark_list"][:], offs)
        for q in range(4):
            nc.sync.dma_start(
                out=tab_s[32 * q : 32 * q + 8, :].bitcast(I32),
                in_=tab_scales[:, 4 * q : 4 * q + 4, :].bitcast(I32),
            )
        load_table(1)
        nc.sync.dma_start(out=ws_w_raw[:].bitcast(I32), in_=ws_words.rearrange("a p c -> p a c").bitcast(I32))
        for r in range(4):
            nc.sync.dma_start(
                out=ws_s_raw[r:P:32, :, :].bitcast(I32),
                in_=ws_scales.rearrange("a (q r) c -> r q a c", r=4)[r].bitcast(I32),
            )
        load_weight("wm", wm, 0, 0)
        nc.sync.dma_start(lists["part_list"][:], offs3)
        load_weight("wm", wm, 1, 0)
        for b in range(2):
            load_gain(b)
        for name, w, b in (("wr", wr, 0), ("wm", wm, 1), ("wr", wr, 1)):
            for a in range(2):
                load_weight(name, w, a, b)
        for a in range(2):
            load_weight("wo", wo, a, 0)

        picked_w, picked_s = {}, {}

        def gather_words(name, a):
            picked_w[name, a] = new([P, S], U32, "%s_w%d" % (name, a))
            nc.vector.tensor_copy(picked_w[name, a][:], tab_w[a][:].bitcast(U32).indirect(lists[name + "_list"][:]))

        def gather_scales(name):
            picked_s[name] = new([P, S], U8, name + "_s")
            nc.vector.tensor_copy(picked_s[name][:], tab_s[:].indirect(lists[name + "_list"][:]))

        codes, scales = {}, {}

        def copy_on(engine, dst, src):
            if engine == "v":
                nc.vector.tensor_copy(out=dst, in_=src)
            else:
                nc.scalar.copy(out=dst, in_=src)

        def quantise_weight(name, a, b, engines):
            grouped = ring.tile([P, PACK * KP], BF16, name="grouped", align_bytes=64)
            if name == "wo":
                dst = grouped[:].rearrange("p (m i j) -> p m j i", i=4, j=PACK)
                src = raw[name, a, b][:].rearrange("p j (m i) -> p m j i", i=4)
                copy_on(engines[0], dst, src)
            else:
                dst = grouped[:].rearrange("p (t q h i j) -> p t q h j i", t=PACK, h=2, i=4, j=PACK)
                src = raw[name, a, b][:].rearrange("p j (q t h i) -> p t q h j i", t=PACK, h=2, i=4)
                for t in range(PACK):
                    copy_on(engines[t % len(engines)], dst[:, t], src[:, t])
            codes[name, a, b] = new([P, KP], U32, "codes_%s%d%d" % (name, a, b))
            scales[name, a, b] = new([P, KP], U8, "scales_%s%d%d" % (name, a, b))
            nc.vector.quantize_mx(out=codes[name, a, b][:].bitcast(FP8X4), scales=scales[name, a, b][:], in_=grouped[:])

        def first_product(dst, name, b, t, cols):
            for a in range(2):
                if name == "sell":
                    c0 = KP * b + P * t
                    lhs = ws_w[:, a, 2 * c0 : 2 * (c0 + P)].bitcast(FP4X4)
                    lhs_scale = ws_s[:, a, c0 : c0 + P]
                    rhs_scale = (picked_s["sell"], sell_s1)[a][:, cols]
                else:
                    w = "wm" if name == "mark" else "wr"
                    lhs = codes[w, a, b][:, P * t : P * (t + 1)].bitcast(FP8X4)
                    lhs_scale = scales[w, a, b][:, P * t : P * (t + 1)]
                    rhs_scale = picked_s[name][4 * a :, cols]
                nc.tensor.matmul_mx(
                    out=dst, lhsT=lhs, lhsT_scale=lhs_scale,
                    rhs=picked_w[name, a][:, cols].bitcast(FP8X4), rhs_scale=rhs_scale,
                    start=(a == 0), stop=(a == 1),
                )

        def bank():
            return psum.tile([P, S], F32, name="bank", bufs=8)

        sell = [new([P, PACK, S], F32, "sell%d" % b) for b in range(2)]
        upper = [new([P, PACK, S], F32, "upper%d" % b) for b in range(2)]

        def sell_half(b):
            for t in range(PACK):
                acc = bank()
                first_product(acc[:], "sell", b, t, slice(0, S))
                nc.scalar.copy(out=sell[b][:, t, :], in_=acc[:])

        def upper_half(b):
            for t in range(PACK):
                acc = bank()
                first_product(acc[:], "mark", b, t, slice(0, S))
                nc.vector.tensor_tensor(upper[b][:, t, :], acc[:], sell[b][:, t, :], ALU.max)

        h_codes, h_scales = {}, {}

        def hidden(b, j0, width, engine):
            cols = slice(j0, j0 + width)
            per_bank = S // width
            lower = new([P, PACK, width], F32, "lower%d_%d" % (b, j0))
            planes = new([P, PACK, width], BF16, "planes%d_%d" % (b, j0))
            for t0 in range(0, PACK, per_bank):
                acc = bank()
                for u in range(per_bank):
                    first_product(acc[:, u * width : (u + 1) * width], "part", b, t0 + u, cols)
                nc.vector.tensor_tensor(
                    lower[:, t0 : t0 + per_bank, :], acc[:].rearrange("p (u c) -> p u c", u=per_bank),
                    sell[b][:, t0 : t0 + per_bank, cols], ALU.min,
                )
            for t in range(PACK):
                nc.vector.scalar_tensor_tensor(
                    planes[:, t, :], upper[b][:, t, cols], gains[:, PACK * b + t : PACK * b + t + 1], lower[:, t, :], ALU.mult, ALU.mult
                )
            woven = new([P, PACK * width], BF16, "woven%d_%d" % (b, j0))
            copy_on(
                engine,
                woven[:].rearrange("p (c i t) -> p c t i", i=4, t=PACK),
                planes[:].rearrange("p t (c i) -> p c t i", i=4),
            )
            made_codes = new([P, width], U32, "h_codes%d_%d" % (b, j0))
            made_scales = new([P, width], U8, "h_scales%d_%d" % (b, j0))
            nc.vector.quantize_mx(out=made_codes[:].bitcast(FP8X4), scales=made_scales[:], in_=woven[:])
            h_codes[b, j0], h_scales[b, j0] = made_codes, made_scales

        out_banks = {}

        def second_product(b, j0, width):
            per_bank = S // width
            made_at = j0 if b == 1 else 0
            cols = slice(j0 - made_at, j0 - made_at + width)
            for n0 in range(0, N // P, per_bank):
                if b == 0:
                    out_banks[j0, n0] = bank()[:].rearrange("p (u c) -> p u c", u=per_bank)
                for u in range(per_bank):
                    n_cols = slice(P * (n0 + u), P * (n0 + u + 1))
                    nc.tensor.matmul_mx(
                        out=out_banks[j0, n0][:, u, :],
                        lhsT=codes["wo", b, 0][:, n_cols].bitcast(FP8X4), lhsT_scale=scales["wo", b, 0][:, n_cols],
                        rhs=h_codes[b, made_at][:, cols].bitcast(FP8X4), rhs_scale=h_scales[b, made_at][:, cols],
                        start=(b == 0 and u == 0), stop=(b == 1 and u == per_bank - 1),
                    )

        def store(j0, width, engines):
            per_bank = S // width
            for n0, engine in zip(range(0, N // P, per_bank), engines):
                result = new([P, per_bank, width], F32, "result%d_%d" % (j0, n0))
                copy_on(engine, result[:], out_banks[j0, n0])
                rows = out[P * n0 : P * (n0 + per_bank), j0 : j0 + width]
                nc.sync.dma_start(out=rows.rearrange("(u p) c -> p u c", u=per_bank), in_=result[:])

        turned = bank()
        nc.tensor.transpose(turned[:, 0:P], gain_rows[:], identity[:])
        nc.scalar.copy(out=gains[:], in_=turned[:, 0 : 2 * PACK])

        gather_words("sell", 0)
        gather_scales("sell")
        nc.scalar.dma_start(out=sell_s1[0:100, :].bitcast(I32), in_=picked_s["sell"][4:104, :].bitcast(I32))
        gather_words("mark", 0)
        gather_words("sell", 1)
        nc.vector.tensor_copy(
            out=ws_w[:].rearrange("p a c -> p (a c)").bitcast(I32).rearrange("p (g t q i) -> p g t q i", g=4, t=PACK, i=4),
            in_=ws_w_raw[:].rearrange("p a c -> p (a c)").bitcast(I32).rearrange("p (g q t i) -> p g t q i", g=4, t=PACK, i=4),
        )
        nc.vector.tensor_copy(
            out=ws_s[:].rearrange("p a c -> p (a c)").bitcast(I32).rearrange("p (g t q i) -> p g t q i", g=4, t=PACK, i=2),
            in_=ws_s_raw[:].rearrange("p a c -> p (a c)").bitcast(I32).rearrange("p (g q t i) -> p g t q i", g=4, t=PACK, i=2),
        )
        gather_words("part", 0)
        gather_words("mark", 1)
        gather_scales("mark")
        gather_words("part", 1)
        quantise_weight("wm", 0, 0, "s")
        quantise_weight("wm", 1, 0, "sv")
        quantise_weight("wr", 0, 0, "sv")
        sell_half(0)
        gather_scales("part")
        upper_half(0)
        quantise_weight("wr", 1, 0, "sv")
        sell_half(1)
        quantise_weight("wm", 0, 1, "sv")
        quantise_weight("wm", 1, 1, "sv")
        quantise_weight("wr", 0, 1, "s")
        quantise_weight("wr", 1, 1, "s")
        hidden(0, 0, S, "s")
        upper_half(1)
        quantise_weight("wo", 0, 0, "s")
        quantise_weight("wo", 1, 0, "s")
        hidden(1, 0, HALF, "s")
        second_product(0, 0, HALF)
        second_product(0, HALF, HALF)
        hidden(1, HALF, HALF, "v")
        second_product(1, 0, HALF)
        store(0, HALF, "ss")
        second_product(1, HALF, HALF)
        store(HALF, HALF, "sv")
